import numpy as np
import ml_dtypes


def mxq(x, axis, fmt="e4m3"):
    dtype, down = {"e4m3": (ml_dtypes.float8_e4m3fn, 7), "e5m2": (ml_dtypes.float8_e5m2, 14)}[fmt]
    v = np.moveaxis(np.asarray(x, np.float32).astype(ml_dtypes.bfloat16).astype(np.float64), axis, -1)
    blocks = v.reshape(v.shape[:-1] + (-1, 32))
    amax = np.abs(blocks).max(-1, keepdims=True)
    byte = np.maximum(np.where(amax > 0, np.frexp(amax)[1] - 1 + 127, 0) - down, 1)
    scale = np.exp2(byte - 127.0)
    codes = (blocks / scale).astype(np.float32).astype(dtype).astype(np.float64)
    return np.moveaxis((codes * scale).reshape(v.shape), -1, axis)


WIDE = False


def mx_kscale(k):
    if not WIDE:
        return np.ones(k)
    levels = np.array([10, -10, 5, -5, 0])
    if k % 512:
        return np.exp2(np.random.permutation(np.resize(levels, k // 32))).repeat(32)
    a = np.empty((k // 512, 16))
    for p in range(k // 512):
        a[p, :8] = np.random.permutation(np.resize(levels, 8))
        for g in range(8):
            far = levels[np.abs(levels - a[p, g]) >= 10]
            a[p, g + 8] = far[np.random.randint(len(far))]
    return np.exp2(a.ravel()).repeat(32)


def f64(x):
    return np.asarray(x).astype(np.float64)


def striped(idx):
    return np.tile(idx.reshape(-1, 16).T, (8, 1)).astype(np.uint16)


def unstriped(offs):
    return offs[:16].T.reshape(-1).astype(np.int64)


def gelu(v):
    return 0.5 * v * (1.0 + np.tanh(np.sqrt(2.0 / np.pi) * (v + 0.044715 * v**3)))


K, T, E, C, H, N = 2560, 512, 4, 128, 512, 384


def by_expert(wq, xq):
    return np.concatenate([wq[e].T @ xq[:, e * C:(e + 1) * C] for e in range(E)], axis=1)


def setup_inputs():
    n = np.random.standard_normal
    s = mx_kscale(K)[:, None]
    u = mx_kscale(H)
    return {
        "xT": (n((K, T)) * s).astype(np.float32),
        "w1": (n((E, K, H)) / np.sqrt(K) / s[None] * u[None, None, :]).astype(np.float32),
        "w2": (n((E, H, N)) / np.sqrt(H) / u[None, :, None]).astype(np.float32),
        "gate": np.tile(np.random.uniform(0.2, 1.0, E * C), (N, 1)).astype(np.float32),
        "offs": striped(np.random.permutation(T)[:E * C]),
    }


def reference(xT, w1, w2, gate, offs):
    idx = unstriped(offs)
    xq = mxq(f64(xT)[:, idx], 0, "e4m3")
    h = gelu(by_expert(mxq(f64(w1), 1, "e4m3"), xq))
    y = by_expert(mxq(f64(w2), 1, "e4m3"), mxq(h, 0, "e4m3"))
    out = np.zeros((N, T))
    out[:, idx] = f64(gate) * y
    return out

@@ -1,0 +1,263 @@
+from contextlib import ExitStack
+
+import concourse.mybir as mybir
+
+K, T, E, C, H, N = 2560, 512, 4, 128, 512, 384
+FLOPS = 2 * E * C * (K * H + H * N)
+
+F32 = mybir.dt.float32
+BF16 = mybir.dt.bfloat16
+U32 = mybir.dt.uint32
+U16 = mybir.dt.uint16
+U8 = mybir.dt.uint8
+FP8X4 = mybir.dt.float8_e4m3fn_x4
+GELU = mybir.ActivationFunctionType.Gelu_apprx_tanh
+MULT = mybir.AluOpType.mult
+
+P = 128
+J = 4
+K_PASS = P * J
+PASSES = K // K_PASS
+HT = H // P
+NB = N // P
+LOOKAHEAD = 9
+SCALAR_TILES = (4, 4, 0, 4, 1)
+SCALAR_TILES_LAST = (4, 0, 4, 2, 1)
+
+
+def tile_routed_moe_kernel(tc, xT, w1, w2, gate, offs, out):
+    nc = tc.nc
+    with ExitStack() as ctx:
+        keep = ctx.enter_context(tc.tile_pool(name="keep", bufs=1))
+        rawp = ctx.enter_context(tc.tile_pool(name="rawp", bufs=13))
+        grp = ctx.enter_context(tc.tile_pool(name="grp", bufs=5))
+        wcp = ctx.enter_context(tc.tile_pool(name="wcp", bufs=10))
+        w2p = ctx.enter_context(tc.tile_pool(name="w2p", bufs=4))
+        hp = ctx.enter_context(tc.tile_pool(name="hp", bufs=2))
+        hps = ctx.enter_context(tc.psum_pool(name="hps", bufs=2))
+        lps = ctx.enter_context(tc.psum_pool(name="lps", bufs=1))
+        yps = ctx.enter_context(tc.psum_pool(name="yps", bufs=2))
+
+        offsets = keep.tile([P, T // 16], U16, name="offsets")
+        nc.sync.dma_start(offsets[:], offs)
+
+        x_codes = keep.tile([P, PASSES, T], U32, align_bytes=64, name="x_codes")
+        x_bytes_a = keep.tile([P, T], U8, align_bytes=64, name="x_bytes_a")
+        x_bytes_b = keep.tile([P, T], U8, align_bytes=64, name="x_bytes_b")
+        s_codes = keep.tile([P, PASSES, T], U32, align_bytes=64, name="s_codes")
+        s_bytes_a = keep.tile([P, T], U8, align_bytes=64, name="s_bytes_a")
+        s_bytes_b = keep.tile([P, T], U8, align_bytes=64, name="s_bytes_b")
+        gates = keep.tile([P, NB, (E - 1) * C], F32, name="gates")
+        gates_last = keep.tile([P, NB, C], F32, name="gates_last")
+        windows = [keep.tile([P, T], F32, name="window%d" % b) for b in range(NB)]
+
+        nc.gpsimd.memset(x_bytes_a[:], 0)
+        nc.gpsimd.memset(x_bytes_b[:], 0)
+
+        def load_x(s):
+            raw = rawp.tile([P, J, T], F32, name="raw")
+            nc.sync.dma_start(raw[:], xT[s * K_PASS : (s + 1) * K_PASS, :].rearrange("(p j) t -> p j t", j=J))
+            return raw
+
+        def load_w1(e, s):
+            raw = rawp.tile([P, J, H], F32, name="raw")
+            nc.sync.dma_start(raw[:], w1[e, s * K_PASS : (s + 1) * K_PASS, :].rearrange("(p j) i -> p j i", j=J))
+            return raw
+
+        def load_w2(e):
+            raw = rawp.tile([P, J, N], F32, name="raw")
+            nc.sync.dma_start(raw[:], w2[e].rearrange("(p j) n -> p j n", j=J))
+            return raw
+
+        def load_gate(last):
+            view = gate.rearrange("(b p) s -> p b s", p=P)
+            if last:
+                nc.sync.dma_start(gates_last[:], view[:, :, (E - 1) * C :])
+            else:
+                nc.sync.dma_start(gates[:], view[:, :, : (E - 1) * C])
+
+        def copy_x(s, raw):
+            g = grp.tile([P, T, J], BF16, align_bytes=64, name="grouped")
+            cut = T // 2 if s == 0 else T
+            nc.scalar.copy(g[:, :cut, :], raw[:, :, :cut].rearrange("p j t -> p t j"))
+            if cut < T:
+                nc.vector.tensor_copy(g[:, cut:, :], raw[:, :, cut:].rearrange("p j t -> p t j"))
+            return g
+
+        def quant_x(s, g):
+            plane = x_bytes_a[4 * s : P, :] if s < 4 else x_bytes_b[:]
+            nc.vector.quantize_mx(x_codes[:, s, :].bitcast(FP8X4), plane, g[:].rearrange("p t j -> p (t j)"))
+
+        def gather_words(s):
+            half = T // 2
+            for a in range(2):
+                nc.vector.tensor_copy(
+                    s_codes[:, s, a * half : (a + 1) * half],
+                    x_codes[:, s, :].indirect(offsets[:, a * half // 16 : (a + 1) * half // 16]),
+                )
+
+        def gather_bytes(dst, src):
+            half = T // 2
+            for a in range(2):
+                nc.vector.tensor_copy(
+                    dst[:, a * half : (a + 1) * half],
+                    src[:].indirect(offsets[:, a * half // 16 : (a + 1) * half // 16]),
+                )
+
+        def copy_w1(e, s, raw):
+            g = grp.tile([P, HT, P, J], BF16, align_bytes=64, name="grouped")
+            cut = SCALAR_TILES_LAST[s] if e == E - 1 else SCALAR_TILES[s]
+            dst = g[:].rearrange("p t m j -> p m t j")
+            src = raw[:].rearrange("p j (m t) -> p m t j", t=HT)
+            if cut > 0:
+                nc.scalar.copy(dst[:, :, :cut, :], src[:, :, :cut, :])
+            if cut < HT:
+                nc.vector.tensor_copy(dst[:, :, cut:, :], src[:, :, cut:, :])
+            return g
+
+        def quant_w1(g):
+            codes = wcp.tile([P, H], U32, align_bytes=64, name="w1_codes")
+            scales = wcp.tile([P, H], U8, align_bytes=64, name="w1_scales")
+            nc.vector.quantize_mx(codes[:].bitcast(FP8X4), scales[:], g[:].rearrange("p t m j -> p (t m j)"))
+            return codes, scales
+
+        def copy_w2(e, raw):
+            g = grp.tile([P, N, J], BF16, align_bytes=64, name="grouped")
+            cut = P if e == E - 1 else N
+            nc.scalar.copy(g[:, :cut, :], raw[:, :, :cut].rearrange("p j n -> p n j"))
+            if cut < N:
+                nc.vector.tensor_copy(g[:, cut:, :], raw[:, :, cut:].rearrange("p j n -> p n j"))
+            return g
+
+        def quant_w2(g):
+            codes = w2p.tile([P, N], U32, align_bytes=64, name="w2_codes")
+            scales = w2p.tile([P, N], U8, align_bytes=64, name="w2_scales")
+            for a, b in ((0, 2 * P), (2 * P, 3 * P)):
+                nc.vector.quantize_mx(
+                    codes[:, a:b].bitcast(FP8X4), scales[:, a:b], g[:, a:b, :].rearrange("p n j -> p (n j)")
+                )
+            return codes, scales
+
+        def slot_scales(s, e):
+            cols = slice(e * C, (e + 1) * C)
+            return s_bytes_a[4 * s : P, cols] if s < 4 else s_bytes_b[:, cols]
+
+        def matmul1(dst, e, s, t, wq):
+            nc.tensor.matmul_mx(
+                dst,
+                lhsT=wq[0][:, t * P : (t + 1) * P].bitcast(FP8X4),
+                lhsT_scale=wq[1][:, t * P : (t + 1) * P],
+                rhs=s_codes[:, s, e * C : (e + 1) * C].bitcast(FP8X4),
+                rhs_scale=slot_scales(s, e),
+                start=(s == 0),
+                stop=(s == PASSES - 1),
+            )
+
+        def hidden(bank):
+            hg = hp.tile([P, C, HT], BF16, align_bytes=64, name="hg")
+            nc.scalar.activation(hg[:], bank[:].rearrange("p t c -> p c t"), GELU)
+            return quant_h(hg)
+
+        def hidden_last(banks):
+            h = hp.tile([P, HT, C], BF16, name="h")
+            for t in range(HT):
+                nc.scalar.activation(h[:, t, :], banks[t][:], GELU)
+            hg = hp.tile([P, C, HT], BF16, align_bytes=64, name="hg")
+            nc.vector.tensor_copy(hg[:], h[:].rearrange("p t c -> p c t"))
+            return quant_h(hg)
+
+        def quant_h(hg):
+            codes = hp.tile([P, C], U32, align_bytes=64, name="h_codes")
+            scales = hp.tile([P, C], U8, align_bytes=64, name="h_scales")
+            nc.vector.quantize_mx(codes[:].bitcast(FP8X4), scales[:], hg[:].rearrange("p c t -> p (c t)"))
+            return codes, scales
+
+        def second(e, w2q, hq):
+            y_ps = yps.tile([P, NB, C], F32, name="y_ps")
+            y = hp.tile([P, NB, C], F32, name="y")
+            for b in range(NB):
+                nc.tensor.matmul_mx(
+                    y_ps[:, b, :],
+                    lhsT=w2q[0][:, b * P : (b + 1) * P].bitcast(FP8X4),
+                    lhsT_scale=w2q[1][:, b * P : (b + 1) * P],
+                    rhs=hq[0][:].bitcast(FP8X4),
+                    rhs_scale=hq[1][:],
+                    start=True,
+                    stop=True,
+                )
+            if e < E - 1:
+                nc.scalar.copy(y[:], y_ps[:])
+                factors = gates[:, :, e * C : (e + 1) * C]
+            else:
+                for b in range(NB):
+                    nc.scalar.copy(y[:, b, :], y_ps[:, b, :])
+                factors = gates_last[:]
+            for b in range(NB):
+                nc.vector.tensor_tensor(
+                    windows[b][:].indirect(offsets[:, e * C // 16 : (e + 1) * C // 16]),
+                    y[:, b, :],
+                    factors[:, b, :],
+                    MULT,
+                )
+
+        jobs = [("x", s) for s in range(PASSES)]
+        for e in range(E):
+            jobs += [("w1", e, s) for s in range(PASSES)]
+            if e == 1:
+                jobs.append(("gate", False))
+            jobs.append(("w2", e))
+        jobs.insert(len(jobs), ("gate", True))
+
+        raws = {}
+
+        def load(i):
+            if i >= len(jobs):
+                return
+            job = jobs[i]
+            if job[0] == "x":
+                raws[i] = load_x(job[1])
+            elif job[0] == "w1":
+                raws[i] = load_w1(job[1], job[2])
+            elif job[0] == "w2":
+                raws[i] = load_w2(job[1])
+            else:
+                load_gate(job[1])
+
+        for i in range(LOOKAHEAD):
+            load(i)
+        w1q = []
+        banks = []
+        hq = None
+        for i, job in enumerate(jobs):
+            load(i + LOOKAHEAD)
+            if job[0] == "x":
+                s = job[1]
+                quant_x(s, copy_x(s, raws.pop(i)))
+                gather_words(s)
+                if s == 3:
+                    gather_bytes(s_bytes_a, x_bytes_a)
+                if s == 4:
+                    gather_bytes(s_bytes_b, x_bytes_b)
+            elif job[0] == "w1":
+                e, s = job[1], job[2]
+                wq = quant_w1(copy_w1(e, s, raws.pop(i)))
+                if e < E - 1:
+                    w1q.append(wq)
+                    if s == PASSES - 1:
+                        bank = hps.tile([P, HT, C], F32, name="h_ps")
+                        for t in range(HT):
+                            for q in range(PASSES):
+                                matmul1(bank[:, t, :], e, q, t, w1q[q])
+                        w1q = []
+                        hq = hidden(bank)
+                else:
+                    if s == 0:
+                        banks = [lps.tile([P, C], F32, name="last_ps%d" % t) for t in range(HT)]
+                    for t in range(HT):
+                        matmul1(banks[t][:], e, s, t, wq)
+                    if s == PASSES - 1:
+                        hq = hidden_last(banks)
+            elif job[0] == "w2":
+                second(job[1], quant_w2(copy_w2(job[1], raws.pop(i))), hq)
+        for b in range(NB):
+            nc.sync.dma_start(out[b * P : (b + 1) * P, :], windows[b][:])

@@ -20,18 +20,19 @@ K_PASS = P * J
 PASSES = K // K_PASS
 HT = H // P
 NB = N // P
-LOOKAHEAD = 9
-SCALAR_TILES = (4, 4, 0, 4, 1)
-SCALAR_TILES_LAST = (4, 0, 4, 2, 1)
+LOOKAHEAD = 3
+SCALAR_TILES = (4, 0, 4, 0, 4)
+SCALAR_TILES_LAST = (4, 0, 4, 0, 1)
+SCALAR_X = (256, 512, 512, 0, 512)
 
 
 def tile_routed_moe_kernel(tc, xT, w1, w2, gate, offs, out):
     nc = tc.nc
     with ExitStack() as ctx:
         keep = ctx.enter_context(tc.tile_pool(name="keep", bufs=1))
-        rawp = ctx.enter_context(tc.tile_pool(name="rawp", bufs=13))
-        grp = ctx.enter_context(tc.tile_pool(name="grp", bufs=5))
-        wcp = ctx.enter_context(tc.tile_pool(name="wcp", bufs=10))
+        rawp = ctx.enter_context(tc.tile_pool(name="rawp", bufs=4))
+        grp = ctx.enter_context(tc.tile_pool(name="grp", bufs=3))
+        wcp = ctx.enter_context(tc.tile_pool(name="wcp", bufs=6))
         w2p = ctx.enter_context(tc.tile_pool(name="w2p", bufs=4))
         hp = ctx.enter_context(tc.tile_pool(name="hp", bufs=2))
         hps = ctx.enter_context(tc.psum_pool(name="hps", bufs=2))
@@ -39,8 +40,6 @@ def tile_routed_moe_kernel(tc, xT, w1, w2, gate, offs, out):
         yps = ctx.enter_context(tc.psum_pool(name="yps", bufs=2))
 
         offsets = keep.tile([P, T // 16], U16, name="offsets")
-        nc.sync.dma_start(offsets[:], offs)
-
         x_codes = keep.tile([P, PASSES, T], U32, align_bytes=64, name="x_codes")
         x_bytes_a = keep.tile([P, T], U8, align_bytes=64, name="x_bytes_a")
         x_bytes_b = keep.tile([P, T], U8, align_bytes=64, name="x_bytes_b")
@@ -76,12 +75,17 @@ def tile_routed_moe_kernel(tc, xT, w1, w2, gate, offs, out):
             else:
                 nc.sync.dma_start(gates[:], view[:, :, : (E - 1) * C])
 
+        def interleave(g, raw, cut, width):
+            for engine_copy, a, b in ((nc.scalar.copy, 0, cut), (nc.vector.tensor_copy, cut, width)):
+                if a < b:
+                    engine_copy(
+                        g[:, a:b, :].rearrange("p (c i) j -> p c j i", i=4),
+                        raw[:, :, a:b].rearrange("p j (c i) -> p c j i", i=4),
+                    )
+
         def copy_x(s, raw):
             g = grp.tile([P, T, J], BF16, align_bytes=64, name="grouped")
-            cut = T // 2 if s == 0 else T
-            nc.scalar.copy(g[:, :cut, :], raw[:, :, :cut].rearrange("p j t -> p t j"))
-            if cut < T:
-                nc.vector.tensor_copy(g[:, cut:, :], raw[:, :, cut:].rearrange("p j t -> p t j"))
+            interleave(g, raw, SCALAR_X[s], T)
             return g
 
         def quant_x(s, g):
@@ -107,12 +111,12 @@ def tile_routed_moe_kernel(tc, xT, w1, w2, gate, offs, out):
         def copy_w1(e, s, raw):
             g = grp.tile([P, HT, P, J], BF16, align_bytes=64, name="grouped")
             cut = SCALAR_TILES_LAST[s] if e == E - 1 else SCALAR_TILES[s]
-            dst = g[:].rearrange("p t m j -> p m t j")
-            src = raw[:].rearrange("p j (m t) -> p m t j", t=HT)
+            dst = g[:].rearrange("p t m j -> p m j t")
+            src = raw[:].rearrange("p j (m t) -> p m j t", t=HT)
             if cut > 0:
-                nc.scalar.copy(dst[:, :, :cut, :], src[:, :, :cut, :])
+                nc.scalar.copy(dst[:, :, :, :cut], src[:, :, :, :cut])
             if cut < HT:
-                nc.vector.tensor_copy(dst[:, :, cut:, :], src[:, :, cut:, :])
+                nc.vector.tensor_copy(dst[:, :, :, cut:], src[:, :, :, cut:])
             return g
 
         def quant_w1(g):
@@ -124,9 +128,7 @@ def tile_routed_moe_kernel(tc, xT, w1, w2, gate, offs, out):
         def copy_w2(e, raw):
             g = grp.tile([P, N, J], BF16, align_bytes=64, name="grouped")
             cut = P if e == E - 1 else N
-            nc.scalar.copy(g[:, :cut, :], raw[:, :, :cut].rearrange("p j n -> p n j"))
-            if cut < N:
-                nc.vector.tensor_copy(g[:, cut:, :], raw[:, :, cut:].rearrange("p j n -> p n j"))
+            interleave(g, raw, cut, N)
             return g
 
         def quant_w2(g):
@@ -203,7 +205,7 @@ def tile_routed_moe_kernel(tc, xT, w1, w2, gate, offs, out):
         jobs = [("x", s) for s in range(PASSES)]
         for e in range(E):
             jobs += [("w1", e, s) for s in range(PASSES)]
-            if e == 1:
+            if e == 0:
                 jobs.append(("gate", False))
             jobs.append(("w2", e))
         jobs.insert(len(jobs), ("gate", True))
@@ -223,7 +225,9 @@ def tile_routed_moe_kernel(tc, xT, w1, w2, gate, offs, out):
             else:
                 load_gate(job[1])
 
-        for i in range(LOOKAHEAD):
+        load(0)
+        nc.sync.dma_start(offsets[:], offs)
+        for i in range(1, LOOKAHEAD):
             load(i)
         w1q = []
         banks = []

@@ -20,7 +20,7 @@ K_PASS = P * J
 PASSES = K // K_PASS
 HT = H // P
 NB = N // P
-LOOKAHEAD = 3
+LOOKAHEAD = 7
 SCALAR_TILES = (4, 0, 4, 0, 4)
 SCALAR_TILES_LAST = (4, 0, 4, 0, 1)
 SCALAR_X = (256, 512, 512, 0, 512)
@@ -30,7 +30,7 @@ def tile_routed_moe_kernel(tc, xT, w1, w2, gate, offs, out):
     nc = tc.nc
     with ExitStack() as ctx:
         keep = ctx.enter_context(tc.tile_pool(name="keep", bufs=1))
-        rawp = ctx.enter_context(tc.tile_pool(name="rawp", bufs=4))
+        rawp = ctx.enter_context(tc.tile_pool(name="rawp", bufs=9))
         grp = ctx.enter_context(tc.tile_pool(name="grp", bufs=3))
         wcp = ctx.enter_context(tc.tile_pool(name="wcp", bufs=6))
         w2p = ctx.enter_context(tc.tile_pool(name="w2p", bufs=4))
@@ -229,14 +229,19 @@ def tile_routed_moe_kernel(tc, xT, w1, w2, gate, offs, out):
         nc.sync.dma_start(offsets[:], offs)
         for i in range(1, LOOKAHEAD):
             load(i)
-        w1q = []
-        banks = []
-        hq = None
-        for i, job in enumerate(jobs):
-            load(i + LOOKAHEAD)
+        state = {"w1q": [], "banks": [], "hq": None}
+
+        def grouped_copy(job, raw):
+            if job[0] == "x":
+                return copy_x(job[1], raw)
+            if job[0] == "w1":
+                return copy_w1(job[1], job[2], raw)
+            return copy_w2(job[1], raw)
+
+        def finish(job, g):
             if job[0] == "x":
                 s = job[1]
-                quant_x(s, copy_x(s, raws.pop(i)))
+                quant_x(s, g)
                 gather_words(s)
                 if s == 3:
                     gather_bytes(s_bytes_a, x_bytes_a)
@@ -244,24 +249,35 @@ def tile_routed_moe_kernel(tc, xT, w1, w2, gate, offs, out):
                     gather_bytes(s_bytes_b, x_bytes_b)
             elif job[0] == "w1":
                 e, s = job[1], job[2]
-                wq = quant_w1(copy_w1(e, s, raws.pop(i)))
+                wq = quant_w1(g)
                 if e < E - 1:
-                    w1q.append(wq)
+                    state["w1q"].append(wq)
                     if s == PASSES - 1:
                         bank = hps.tile([P, HT, C], F32, name="h_ps")
                         for t in range(HT):
                             for q in range(PASSES):
-                                matmul1(bank[:, t, :], e, q, t, w1q[q])
-                        w1q = []
-                        hq = hidden(bank)
+                                matmul1(bank[:, t, :], e, q, t, state["w1q"][q])
+                        state["w1q"] = []
+                        state["hq"] = hidden(bank)
                 else:
                     if s == 0:
-                        banks = [lps.tile([P, C], F32, name="last_ps%d" % t) for t in range(HT)]
+                        state["banks"] = [lps.tile([P, C], F32, name="last_ps%d" % t) for t in range(HT)]
                     for t in range(HT):
-                        matmul1(banks[t][:], e, s, t, wq)
+                        matmul1(state["banks"][t][:], e, s, t, wq)
                     if s == PASSES - 1:
-                        hq = hidden_last(banks)
-            elif job[0] == "w2":
-                second(job[1], quant_w2(copy_w2(job[1], raws.pop(i))), hq)
+                        state["hq"] = hidden_last(state["banks"])
+            else:
+                second(job[1], quant_w2(g), state["hq"])
+
+        pending = None
+        for i, job in enumerate(jobs):
+            load(i + LOOKAHEAD)
+            if job[0] == "gate":
+                continue
+            g = grouped_copy(job, raws.pop(i))
+            if pending is not None:
+                finish(*pending)
+            pending = (job, g)
+        finish(*pending)
         for b in range(NB):
             nc.sync.dma_start(out[b * P : (b + 1) * P, :], windows[b][:])

@@ -20,264 +20,281 @@ K_PASS = P * J
 PASSES = K // K_PASS
 HT = H // P
 NB = N // P
-LOOKAHEAD = 7
+LAST = E - 1
+OFFS_COL = 16
+GATHER = 256
+PLANE = 4
+SHARED = 4
+
+AHEAD = 7
+
+SCALAR_TOKENS = (256, 512, 512, 0, 512)
 SCALAR_TILES = (4, 0, 4, 0, 4)
-SCALAR_TILES_LAST = (4, 0, 4, 0, 1)
-SCALAR_X = (256, 512, 512, 0, 512)
+SCALAR_TILES_LAST = (2, 2, 2, 2)
 
 
 def tile_routed_moe_kernel(tc, xT, w1, w2, gate, offs, out):
     nc = tc.nc
     with ExitStack() as ctx:
         keep = ctx.enter_context(tc.tile_pool(name="keep", bufs=1))
-        rawp = ctx.enter_context(tc.tile_pool(name="rawp", bufs=9))
-        grp = ctx.enter_context(tc.tile_pool(name="grp", bufs=3))
-        wcp = ctx.enter_context(tc.tile_pool(name="wcp", bufs=6))
-        w2p = ctx.enter_context(tc.tile_pool(name="w2p", bufs=4))
-        hp = ctx.enter_context(tc.tile_pool(name="hp", bufs=2))
-        hps = ctx.enter_context(tc.psum_pool(name="hps", bufs=2))
-        lps = ctx.enter_context(tc.psum_pool(name="lps", bufs=1))
-        yps = ctx.enter_context(tc.psum_pool(name="yps", bufs=2))
+        raw_ring = ctx.enter_context(tc.tile_pool(name="raw_ring", bufs=AHEAD + 2))
+        group_ring = ctx.enter_context(tc.tile_pool(name="group_ring", bufs=3))
+        w1_ring = ctx.enter_context(tc.tile_pool(name="w1_ring", bufs=PASSES + 1))
+        w2_ring = ctx.enter_context(tc.tile_pool(name="w2_ring", bufs=E))
+        hidden_ring = ctx.enter_context(tc.tile_pool(name="hidden_ring", bufs=2))
+        first_psum = ctx.enter_context(tc.psum_pool(name="first_psum", bufs=2))
+        last_psum = ctx.enter_context(tc.psum_pool(name="last_psum", bufs=1))
+        second_psum = ctx.enter_context(tc.psum_pool(name="second_psum", bufs=2))
 
-        offsets = keep.tile([P, T // 16], U16, name="offsets")
-        x_codes = keep.tile([P, PASSES, T], U32, align_bytes=64, name="x_codes")
-        x_bytes_a = keep.tile([P, T], U8, align_bytes=64, name="x_bytes_a")
-        x_bytes_b = keep.tile([P, T], U8, align_bytes=64, name="x_bytes_b")
-        s_codes = keep.tile([P, PASSES, T], U32, align_bytes=64, name="s_codes")
-        s_bytes_a = keep.tile([P, T], U8, align_bytes=64, name="s_bytes_a")
-        s_bytes_b = keep.tile([P, T], U8, align_bytes=64, name="s_bytes_b")
-        gates = keep.tile([P, NB, (E - 1) * C], F32, name="gates")
+        offsets = keep.tile([P, T // OFFS_COL], U16, name="offsets")
+
+        token_codes = keep.tile([P, PASSES, T], U32, align_bytes=64, name="token_codes")
+        token_scales_shared = keep.tile([P, T], U8, align_bytes=64, name="token_scales_shared")
+        token_scales_own = keep.tile([P, T], U8, align_bytes=64, name="token_scales_own")
+        slot_codes = keep.tile([P, PASSES, T], U32, align_bytes=64, name="slot_codes")
+        slot_scales_shared = keep.tile([P, T], U8, align_bytes=64, name="slot_scales_shared")
+        slot_scales_own = keep.tile([P, T], U8, align_bytes=64, name="slot_scales_own")
+
+        gates = keep.tile([P, NB, LAST * C], F32, name="gates")
         gates_last = keep.tile([P, NB, C], F32, name="gates_last")
         windows = [keep.tile([P, T], F32, name="window%d" % b) for b in range(NB)]
 
-        nc.gpsimd.memset(x_bytes_a[:], 0)
-        nc.gpsimd.memset(x_bytes_b[:], 0)
+        warm = keep.tile([P, 8], F32, name="warm")
+        nc.gpsimd.memset(warm[:], 0.0)
+        nc.scalar.activation(warm[:], warm[:], GELU)
 
-        def load_x(s):
-            raw = rawp.tile([P, J, T], F32, name="raw")
-            nc.sync.dma_start(raw[:], xT[s * K_PASS : (s + 1) * K_PASS, :].rearrange("(p j) t -> p j t", j=J))
+        nc.gpsimd.memset(token_scales_shared[:], 0)
+        nc.gpsimd.memset(token_scales_own[:], 0)
+
+        def scale_rows(s, shared, own):
+            return shared[PLANE * s : P, :] if s < SHARED else own[:]
+
+        def load_rows(rows, width):
+            raw = raw_ring.tile([P, J, width], F32, name="raw")
+            nc.sync.dma_start(raw[:], rows.rearrange("(p j) c -> p j c", j=J))
             return raw
 
-        def load_w1(e, s):
-            raw = rawp.tile([P, J, H], F32, name="raw")
-            nc.sync.dma_start(raw[:], w1[e, s * K_PASS : (s + 1) * K_PASS, :].rearrange("(p j) i -> p j i", j=J))
-            return raw
-
-        def load_w2(e):
-            raw = rawp.tile([P, J, N], F32, name="raw")
-            nc.sync.dma_start(raw[:], w2[e].rearrange("(p j) n -> p j n", j=J))
-            return raw
-
-        def load_gate(last):
-            view = gate.rearrange("(b p) s -> p b s", p=P)
-            if last:
-                nc.sync.dma_start(gates_last[:], view[:, :, (E - 1) * C :])
+        def load(chunk):
+            kind, e, s = chunk
+            k_rows = slice(s * K_PASS, (s + 1) * K_PASS)
+            if kind == "x":
+                return load_rows(xT[k_rows, :], T)
+            if kind == "w1":
+                return load_rows(w1[e, k_rows, :], H)
+            if kind == "w2":
+                return load_rows(w2[e], N)
+            gate_rows = gate.rearrange("(b p) s -> p b s", p=P)
+            if e == LAST:
+                nc.sync.dma_start(gates_last[:], gate_rows[:, :, LAST * C :])
             else:
-                nc.sync.dma_start(gates[:], view[:, :, : (E - 1) * C])
+                nc.sync.dma_start(gates[:], gate_rows[:, :, : LAST * C])
+            return None
 
-        def interleave(g, raw, cut, width):
-            for engine_copy, a, b in ((nc.scalar.copy, 0, cut), (nc.vector.tensor_copy, cut, width)):
-                if a < b:
-                    engine_copy(
-                        g[:, a:b, :].rearrange("p (c i) j -> p c j i", i=4),
-                        raw[:, :, a:b].rearrange("p j (c i) -> p c j i", i=4),
-                    )
+        def interleave(engine_copy, grouped, raw, first, end):
+            engine_copy(
+                grouped[:, first:end, :].rearrange("p (c i) j -> p c j i", i=4),
+                raw[:, :, first:end].rearrange("p j (c i) -> p c j i", i=4),
+            )
 
-        def copy_x(s, raw):
-            g = grp.tile([P, T, J], BF16, align_bytes=64, name="grouped")
-            interleave(g, raw, SCALAR_X[s], T)
-            return g
+        def group_x(s, raw):
+            grouped = group_ring.tile([P, T, J], BF16, align_bytes=64, name="grouped")
+            cut = SCALAR_TOKENS[s]
+            if cut > 0:
+                interleave(nc.scalar.copy, grouped, raw, 0, cut)
+            if cut < T:
+                interleave(nc.vector.tensor_copy, grouped, raw, cut, T)
+            return grouped
 
-        def quant_x(s, g):
-            plane = x_bytes_a[4 * s : P, :] if s < 4 else x_bytes_b[:]
-            nc.vector.quantize_mx(x_codes[:, s, :].bitcast(FP8X4), plane, g[:].rearrange("p t j -> p (t j)"))
-
-        def gather_words(s):
-            half = T // 2
-            for a in range(2):
-                nc.vector.tensor_copy(
-                    s_codes[:, s, a * half : (a + 1) * half],
-                    x_codes[:, s, :].indirect(offsets[:, a * half // 16 : (a + 1) * half // 16]),
-                )
-
-        def gather_bytes(dst, src):
-            half = T // 2
-            for a in range(2):
-                nc.vector.tensor_copy(
-                    dst[:, a * half : (a + 1) * half],
-                    src[:].indirect(offsets[:, a * half // 16 : (a + 1) * half // 16]),
-                )
-
-        def copy_w1(e, s, raw):
-            g = grp.tile([P, HT, P, J], BF16, align_bytes=64, name="grouped")
-            cut = SCALAR_TILES_LAST[s] if e == E - 1 else SCALAR_TILES[s]
-            dst = g[:].rearrange("p t m j -> p m j t")
+        def group_w1(e, s, raw):
+            grouped = group_ring.tile([P, HT, P, J], BF16, align_bytes=64, name="grouped")
+            dst = grouped[:].rearrange("p t m j -> p m j t")
             src = raw[:].rearrange("p j (m t) -> p m j t", t=HT)
+            if e == LAST and s == PASSES - 1:
+                nc.vector.tensor_copy(dst[:, :, :, :2], src[:, :, :, :2])
+                nc.scalar.copy(dst[:, :, :, 3:], src[:, :, :, 3:])
+                nc.vector.tensor_copy(dst[:, :, :, 2:3], src[:, :, :, 2:3])
+                return grouped
+            cut = SCALAR_TILES_LAST[s] if e == LAST else SCALAR_TILES[s]
             if cut > 0:
                 nc.scalar.copy(dst[:, :, :, :cut], src[:, :, :, :cut])
             if cut < HT:
                 nc.vector.tensor_copy(dst[:, :, :, cut:], src[:, :, :, cut:])
-            return g
+            return grouped
 
-        def quant_w1(g):
-            codes = wcp.tile([P, H], U32, align_bytes=64, name="w1_codes")
-            scales = wcp.tile([P, H], U8, align_bytes=64, name="w1_scales")
-            nc.vector.quantize_mx(codes[:].bitcast(FP8X4), scales[:], g[:].rearrange("p t m j -> p (t m j)"))
-            return codes, scales
+        def group_w2(e, raw):
+            grouped = group_ring.tile([P, N, J], BF16, align_bytes=64, name="grouped")
+            interleave(nc.vector.tensor_copy if e == LAST else nc.scalar.copy, grouped, raw, 0, N)
+            return grouped
 
-        def copy_w2(e, raw):
-            g = grp.tile([P, N, J], BF16, align_bytes=64, name="grouped")
-            cut = P if e == E - 1 else N
-            interleave(g, raw, cut, N)
-            return g
+        def quantize_x(s, grouped):
+            nc.vector.quantize_mx(
+                token_codes[:, s, :].bitcast(FP8X4),
+                scale_rows(s, token_scales_shared, token_scales_own),
+                grouped[:].rearrange("p t j -> p (t j)"),
+            )
 
-        def quant_w2(g):
-            codes = w2p.tile([P, N], U32, align_bytes=64, name="w2_codes")
-            scales = w2p.tile([P, N], U8, align_bytes=64, name="w2_scales")
-            for a, b in ((0, 2 * P), (2 * P, 3 * P)):
+        def gather(slots, tokens):
+            for first in range(0, T, GATHER):
+                end = first + GATHER
+                list_cols = offsets[:, first // OFFS_COL : end // OFFS_COL]
+                nc.vector.tensor_copy(slots[:, first:end], tokens.indirect(list_cols))
+
+        def quantize_w1(grouped, parts):
+            codes = w1_ring.tile([P, H], U32, align_bytes=64, name="w1_codes")
+            scales = w1_ring.tile([P, H], U8, align_bytes=64, name="w1_scales")
+            step = HT // parts
+            for t in range(0, HT, step):
+                cols = slice(t * P, (t + step) * P)
                 nc.vector.quantize_mx(
-                    codes[:, a:b].bitcast(FP8X4), scales[:, a:b], g[:, a:b, :].rearrange("p n j -> p (n j)")
+                    codes[:, cols].bitcast(FP8X4),
+                    scales[:, cols],
+                    grouped[:, t : t + step, :, :].rearrange("p t m j -> p (t m j)"),
                 )
             return codes, scales
 
-        def slot_scales(s, e):
-            cols = slice(e * C, (e + 1) * C)
-            return s_bytes_a[4 * s : P, cols] if s < 4 else s_bytes_b[:, cols]
+        def quantize_w2(grouped):
+            codes = w2_ring.tile([P, N], U32, align_bytes=64, name="w2_codes")
+            scales = w2_ring.tile([P, N], U8, align_bytes=64, name="w2_scales")
+            for first, end in ((0, 2 * P), (2 * P, N)):
+                nc.vector.quantize_mx(
+                    codes[:, first:end].bitcast(FP8X4),
+                    scales[:, first:end],
+                    grouped[:, first:end, :].rearrange("p n j -> p (n j)"),
+                )
+            return codes, scales
 
-        def matmul1(dst, e, s, t, wq):
+        def quantize_h(grouped):
+            codes = hidden_ring.tile([P, C], U32, align_bytes=64, name="h_codes")
+            scales = hidden_ring.tile([P, C], U8, align_bytes=64, name="h_scales")
+            nc.vector.quantize_mx(
+                codes[:].bitcast(FP8X4), scales[:], grouped[:].rearrange("p c t -> p (c t)")
+            )
+            return codes, scales
+
+        def first_product(sums, e, s, t, w1_mx):
+            codes, scales = w1_mx
+            cols = slice(t * P, (t + 1) * P)
+            slots = slice(e * C, (e + 1) * C)
             nc.tensor.matmul_mx(
-                dst,
-                lhsT=wq[0][:, t * P : (t + 1) * P].bitcast(FP8X4),
-                lhsT_scale=wq[1][:, t * P : (t + 1) * P],
-                rhs=s_codes[:, s, e * C : (e + 1) * C].bitcast(FP8X4),
-                rhs_scale=slot_scales(s, e),
+                sums,
+                lhsT=codes[:, cols].bitcast(FP8X4),
+                lhsT_scale=scales[:, cols],
+                rhs=slot_codes[:, s, slots].bitcast(FP8X4),
+                rhs_scale=scale_rows(s, slot_scales_shared, slot_scales_own)[:, slots],
                 start=(s == 0),
                 stop=(s == PASSES - 1),
             )
 
-        def hidden(bank):
-            hg = hp.tile([P, C, HT], BF16, align_bytes=64, name="hg")
-            nc.scalar.activation(hg[:], bank[:].rearrange("p t c -> p c t"), GELU)
-            return quant_h(hg)
+        def hidden(e, w1_mx):
+            bank = first_psum.tile([P, HT, C], F32, name="first_sums")
+            for t in range(HT):
+                for s in range(PASSES):
+                    first_product(bank[:, t, :], e, s, t, w1_mx[s])
+            grouped = hidden_ring.tile([P, C, HT], BF16, align_bytes=64, name="h_grouped")
+            nc.scalar.activation(grouped[:], bank[:].rearrange("p t c -> p c t"), GELU)
+            return quantize_h(grouped)
 
         def hidden_last(banks):
-            h = hp.tile([P, HT, C], BF16, name="h")
+            h = hidden_ring.tile([P, HT, C], BF16, name="h")
             for t in range(HT):
                 nc.scalar.activation(h[:, t, :], banks[t][:], GELU)
-            hg = hp.tile([P, C, HT], BF16, align_bytes=64, name="hg")
-            nc.vector.tensor_copy(hg[:], h[:].rearrange("p t c -> p c t"))
-            return quant_h(hg)
+            grouped = hidden_ring.tile([P, C, HT], BF16, align_bytes=64, name="h_grouped")
+            nc.vector.tensor_copy(grouped[:], h[:].rearrange("p t c -> p c t"))
+            return quantize_h(grouped)
 
-        def quant_h(hg):
-            codes = hp.tile([P, C], U32, align_bytes=64, name="h_codes")
-            scales = hp.tile([P, C], U8, align_bytes=64, name="h_scales")
-            nc.vector.quantize_mx(codes[:].bitcast(FP8X4), scales[:], hg[:].rearrange("p c t -> p (c t)"))
-            return codes, scales
-
-        def second(e, w2q, hq):
-            y_ps = yps.tile([P, NB, C], F32, name="y_ps")
-            y = hp.tile([P, NB, C], F32, name="y")
+        def second_product(e, w2_mx, h_mx):
+            codes, scales = w2_mx
+            if e == LAST:
+                sums = [last_psum.tile([P, C], F32, name="last_sums%d" % b)[:] for b in range(NB)]
+            else:
+                bank = second_psum.tile([P, NB, C], F32, name="second_sums")
+                sums = [bank[:, b, :] for b in range(NB)]
+            y = hidden_ring.tile([P, NB, C], F32, name="y")
             for b in range(NB):
+                cols = slice(b * P, (b + 1) * P)
                 nc.tensor.matmul_mx(
-                    y_ps[:, b, :],
-                    lhsT=w2q[0][:, b * P : (b + 1) * P].bitcast(FP8X4),
-                    lhsT_scale=w2q[1][:, b * P : (b + 1) * P],
-                    rhs=hq[0][:].bitcast(FP8X4),
-                    rhs_scale=hq[1][:],
+                    sums[b],
+                    lhsT=codes[:, cols].bitcast(FP8X4),
+                    lhsT_scale=scales[:, cols],
+                    rhs=h_mx[0][:].bitcast(FP8X4),
+                    rhs_scale=h_mx[1][:],
                     start=True,
                     stop=True,
                 )
-            if e < E - 1:
-                nc.scalar.copy(y[:], y_ps[:])
-                factors = gates[:, :, e * C : (e + 1) * C]
-            else:
+            if e == LAST:
                 for b in range(NB):
-                    nc.scalar.copy(y[:, b, :], y_ps[:, b, :])
+                    nc.scalar.copy(y[:, b, :], sums[b])
                 factors = gates_last[:]
+            else:
+                nc.scalar.copy(y[:], bank[:])
+                factors = gates[:, :, e * C : (e + 1) * C]
+            list_cols = offsets[:, e * C // OFFS_COL : (e + 1) * C // OFFS_COL]
             for b in range(NB):
                 nc.vector.tensor_tensor(
-                    windows[b][:].indirect(offsets[:, e * C // 16 : (e + 1) * C // 16]),
-                    y[:, b, :],
-                    factors[:, b, :],
-                    MULT,
+                    windows[b][:].indirect(list_cols), y[:, b, :], factors[:, b, :], MULT
                 )
 
-        jobs = [("x", s) for s in range(PASSES)]
+        chunks = [("x", 0, s) for s in range(PASSES)]
         for e in range(E):
-            jobs += [("w1", e, s) for s in range(PASSES)]
+            chunks += [("w1", e, s) for s in range(PASSES)]
             if e == 0:
-                jobs.append(("gate", False))
-            jobs.append(("w2", e))
-        jobs.insert(len(jobs), ("gate", True))
+                chunks.append(("gate", 0, 0))
+            chunks.append(("w2", e, 0))
+        chunks.append(("gate", LAST, 0))
 
-        raws = {}
+        def group(chunk, raw):
+            kind, e, s = chunk
+            if kind == "x":
+                return group_x(s, raw)
+            if kind == "w1":
+                return group_w1(e, s, raw)
+            return group_w2(e, raw)
 
-        def load(i):
-            if i >= len(jobs):
-                return
-            job = jobs[i]
-            if job[0] == "x":
-                raws[i] = load_x(job[1])
-            elif job[0] == "w1":
-                raws[i] = load_w1(job[1], job[2])
-            elif job[0] == "w2":
-                raws[i] = load_w2(job[1])
+        w1_done = []
+        last_banks = []
+        h_done = []
+
+        def finish(chunk, grouped):
+            kind, e, s = chunk
+            if kind == "x":
+                quantize_x(s, grouped)
+                gather(slot_codes[:, s, :], token_codes[:, s, :])
+                if s == SHARED - 1:
+                    gather(slot_scales_shared, token_scales_shared[:])
+                if s == PASSES - 1:
+                    gather(slot_scales_own, token_scales_own[:])
+            elif kind == "w2":
+                second_product(e, quantize_w2(grouped), h_done[-1])
+            elif e == LAST:
+                w1_mx = quantize_w1(grouped, 2 if s == PASSES - 1 else 1)
+                if s == 0:
+                    last_banks.extend(
+                        [last_psum.tile([P, C], F32, name="last_sums%d" % t) for t in range(HT)]
+                    )
+                for t in range(HT):
+                    first_product(last_banks[t][:], e, s, t, w1_mx)
+                if s == PASSES - 1:
+                    h_done.append(hidden_last(last_banks))
             else:
-                load_gate(job[1])
+                w1_done.append(quantize_w1(grouped, 1))
+                if s == PASSES - 1:
+                    h_done.append(hidden(e, w1_done))
+                    w1_done.clear()
 
-        load(0)
+        raws = [load(chunks[0])]
         nc.sync.dma_start(offsets[:], offs)
-        for i in range(1, LOOKAHEAD):
-            load(i)
-        state = {"w1q": [], "banks": [], "hq": None}
-
-        def grouped_copy(job, raw):
-            if job[0] == "x":
-                return copy_x(job[1], raw)
-            if job[0] == "w1":
-                return copy_w1(job[1], job[2], raw)
-            return copy_w2(job[1], raw)
-
-        def finish(job, g):
-            if job[0] == "x":
-                s = job[1]
-                quant_x(s, g)
-                gather_words(s)
-                if s == 3:
-                    gather_bytes(s_bytes_a, x_bytes_a)
-                if s == 4:
-                    gather_bytes(s_bytes_b, x_bytes_b)
-            elif job[0] == "w1":
-                e, s = job[1], job[2]
-                wq = quant_w1(g)
-                if e < E - 1:
-                    state["w1q"].append(wq)
-                    if s == PASSES - 1:
-                        bank = hps.tile([P, HT, C], F32, name="h_ps")
-                        for t in range(HT):
-                            for q in range(PASSES):
-                                matmul1(bank[:, t, :], e, q, t, state["w1q"][q])
-                        state["w1q"] = []
-                        state["hq"] = hidden(bank)
-                else:
-                    if s == 0:
-                        state["banks"] = [lps.tile([P, C], F32, name="last_ps%d" % t) for t in range(HT)]
-                    for t in range(HT):
-                        matmul1(state["banks"][t][:], e, s, t, wq)
-                    if s == PASSES - 1:
-                        state["hq"] = hidden_last(state["banks"])
-            else:
-                second(job[1], quant_w2(g), state["hq"])
-
+        raws += [load(chunk) for chunk in chunks[1:AHEAD]]
         pending = None
-        for i, job in enumerate(jobs):
-            load(i + LOOKAHEAD)
-            if job[0] == "gate":
+        for i, chunk in enumerate(chunks):
+            if i + AHEAD < len(chunks):
+                raws.append(load(chunks[i + AHEAD]))
+            if chunk[0] == "gate":
                 continue
-            g = grouped_copy(job, raws.pop(i))
+            grouped = group(chunk, raws[i])
             if pending is not None:
                 finish(*pending)
-            pending = (job, g)
+            pending = (chunk, grouped)
         finish(*pending)
+
         for b in range(NB):
             nc.sync.dma_start(out[b * P : (b + 1) * P, :], windows[b][:])

from contextlib import ExitStack

import concourse.mybir as mybir

K, T, E, C, H, N = 2560, 512, 4, 128, 512, 384
FLOPS = 2 * E * C * (K * H + H * N)

F32 = mybir.dt.float32
BF16 = mybir.dt.bfloat16
U32 = mybir.dt.uint32
U16 = mybir.dt.uint16
U8 = mybir.dt.uint8
FP8X4 = mybir.dt.float8_e4m3fn_x4
GELU = mybir.ActivationFunctionType.Gelu_apprx_tanh
MULT = mybir.AluOpType.mult

P = 128
J = 4
K_PASS = P * J
PASSES = K // K_PASS
HT = H // P
NB = N // P
LAST = E - 1
OFFS_COL = 16
GATHER = 256
PLANE = 4
SHARED = 4

AHEAD = 7

SCALAR_TOKENS = (256, 512, 512, 0, 512)
SCALAR_TILES = (4, 0, 4, 0, 4)
SCALAR_TILES_LAST = (2, 2, 2, 2)


def tile_routed_moe_kernel(tc, xT, w1, w2, gate, offs, out):
    nc = tc.nc
    with ExitStack() as ctx:
        keep = ctx.enter_context(tc.tile_pool(name="keep", bufs=1))
        raw_ring = ctx.enter_context(tc.tile_pool(name="raw_ring", bufs=AHEAD + 2))
        group_ring = ctx.enter_context(tc.tile_pool(name="group_ring", bufs=3))
        w1_ring = ctx.enter_context(tc.tile_pool(name="w1_ring", bufs=PASSES + 1))
        w2_ring = ctx.enter_context(tc.tile_pool(name="w2_ring", bufs=E))
        hidden_ring = ctx.enter_context(tc.tile_pool(name="hidden_ring", bufs=2))
        first_psum = ctx.enter_context(tc.psum_pool(name="first_psum", bufs=2))
        last_psum = ctx.enter_context(tc.psum_pool(name="last_psum", bufs=1))
        second_psum = ctx.enter_context(tc.psum_pool(name="second_psum", bufs=2))

        offsets = keep.tile([P, T // OFFS_COL], U16, name="offsets")

        token_codes = keep.tile([P, PASSES, T], U32, align_bytes=64, name="token_codes")
        token_scales_shared = keep.tile([P, T], U8, align_bytes=64, name="token_scales_shared")
        token_scales_own = keep.tile([P, T], U8, align_bytes=64, name="token_scales_own")
        slot_codes = keep.tile([P, PASSES, T], U32, align_bytes=64, name="slot_codes")
        slot_scales_shared = keep.tile([P, T], U8, align_bytes=64, name="slot_scales_shared")
        slot_scales_own = keep.tile([P, T], U8, align_bytes=64, name="slot_scales_own")

        gates = keep.tile([P, NB, LAST * C], F32, name="gates")
        gates_last = keep.tile([P, NB, C], F32, name="gates_last")
        windows = [keep.tile([P, T], F32, name="window%d" % b) for b in range(NB)]

        warm = keep.tile([P, 8], F32, name="warm")
        nc.gpsimd.memset(warm[:], 0.0)
        nc.scalar.activation(warm[:], warm[:], GELU)

        nc.gpsimd.memset(token_scales_shared[:], 0)
        nc.gpsimd.memset(token_scales_own[:], 0)

        def scale_rows(s, shared, own):
            return shared[PLANE * s : P, :] if s < SHARED else own[:]

        def load_rows(rows, width):
            raw = raw_ring.tile([P, J, width], F32, name="raw")
            nc.sync.dma_start(raw[:], rows.rearrange("(p j) c -> p j c", j=J))
            return raw

        def load(chunk):
            kind, e, s = chunk
            k_rows = slice(s * K_PASS, (s + 1) * K_PASS)
            if kind == "x":
                return load_rows(xT[k_rows, :], T)
            if kind == "w1":
                return load_rows(w1[e, k_rows, :], H)
            if kind == "w2":
                return load_rows(w2[e], N)
            gate_rows = gate.rearrange("(b p) s -> p b s", p=P)
            if e == LAST:
                nc.sync.dma_start(gates_last[:], gate_rows[:, :, LAST * C :])
            else:
                nc.sync.dma_start(gates[:], gate_rows[:, :, : LAST * C])
            return None

        def interleave(engine_copy, grouped, raw, first, end):
            engine_copy(
                grouped[:, first:end, :].rearrange("p (c i) j -> p c j i", i=4),
                raw[:, :, first:end].rearrange("p j (c i) -> p c j i", i=4),
            )

        def group_x(s, raw):
            grouped = group_ring.tile([P, T, J], BF16, align_bytes=64, name="grouped")
            cut = SCALAR_TOKENS[s]
            if cut > 0:
                interleave(nc.scalar.copy, grouped, raw, 0, cut)
            if cut < T:
                interleave(nc.vector.tensor_copy, grouped, raw, cut, T)
            return grouped

        def group_w1(e, s, raw):
            grouped = group_ring.tile([P, HT, P, J], BF16, align_bytes=64, name="grouped")
            dst = grouped[:].rearrange("p t m j -> p m j t")
            src = raw[:].rearrange("p j (m t) -> p m j t", t=HT)
            if e == LAST and s == PASSES - 1:
                nc.vector.tensor_copy(dst[:, :, :, :2], src[:, :, :, :2])
                nc.scalar.copy(dst[:, :, :, 3:], src[:, :, :, 3:])
                nc.vector.tensor_copy(dst[:, :, :, 2:3], src[:, :, :, 2:3])
                return grouped
            cut = SCALAR_TILES_LAST[s] if e == LAST else SCALAR_TILES[s]
            if cut > 0:
                nc.scalar.copy(dst[:, :, :, :cut], src[:, :, :, :cut])
            if cut < HT:
                nc.vector.tensor_copy(dst[:, :, :, cut:], src[:, :, :, cut:])
            return grouped

        def group_w2(e, raw):
            grouped = group_ring.tile([P, N, J], BF16, align_bytes=64, name="grouped")
            interleave(nc.vector.tensor_copy if e == LAST else nc.scalar.copy, grouped, raw, 0, N)
            return grouped

        def quantize_x(s, grouped):
            nc.vector.quantize_mx(
                token_codes[:, s, :].bitcast(FP8X4),
                scale_rows(s, token_scales_shared, token_scales_own),
                grouped[:].rearrange("p t j -> p (t j)"),
            )

        def gather(slots, tokens):
            for first in range(0, T, GATHER):
                end = first + GATHER
                list_cols = offsets[:, first // OFFS_COL : end // OFFS_COL]
                nc.vector.tensor_copy(slots[:, first:end], tokens.indirect(list_cols))

        def quantize_w1(grouped, parts):
            codes = w1_ring.tile([P, H], U32, align_bytes=64, name="w1_codes")
            scales = w1_ring.tile([P, H], U8, align_bytes=64, name="w1_scales")
            step = HT // parts
            for t in range(0, HT, step):
                cols = slice(t * P, (t + step) * P)
                nc.vector.quantize_mx(
                    codes[:, cols].bitcast(FP8X4),
                    scales[:, cols],
                    grouped[:, t : t + step, :, :].rearrange("p t m j -> p (t m j)"),
                )
            return codes, scales

        def quantize_w2(grouped):
            codes = w2_ring.tile([P, N], U32, align_bytes=64, name="w2_codes")
            scales = w2_ring.tile([P, N], U8, align_bytes=64, name="w2_scales")
            for first, end in ((0, 2 * P), (2 * P, N)):
                nc.vector.quantize_mx(
                    codes[:, first:end].bitcast(FP8X4),
                    scales[:, first:end],
                    grouped[:, first:end, :].rearrange("p n j -> p (n j)"),
                )
            return codes, scales

        def quantize_h(grouped):
            codes = hidden_ring.tile([P, C], U32, align_bytes=64, name="h_codes")
            scales = hidden_ring.tile([P, C], U8, align_bytes=64, name="h_scales")
            nc.vector.quantize_mx(
                codes[:].bitcast(FP8X4), scales[:], grouped[:].rearrange("p c t -> p (c t)")
            )
            return codes, scales

        def first_product(sums, e, s, t, w1_mx):
            codes, scales = w1_mx
            cols = slice(t * P, (t + 1) * P)
            slots = slice(e * C, (e + 1) * C)
            nc.tensor.matmul_mx(
                sums,
                lhsT=codes[:, cols].bitcast(FP8X4),
                lhsT_scale=scales[:, cols],
                rhs=slot_codes[:, s, slots].bitcast(FP8X4),
                rhs_scale=scale_rows(s, slot_scales_shared, slot_scales_own)[:, slots],
                start=(s == 0),
                stop=(s == PASSES - 1),
            )

        def hidden(e, w1_mx):
            bank = first_psum.tile([P, HT, C], F32, name="first_sums")
            for t in range(HT):
                for s in range(PASSES):
                    first_product(bank[:, t, :], e, s, t, w1_mx[s])
            grouped = hidden_ring.tile([P, C, HT], BF16, align_bytes=64, name="h_grouped")
            nc.scalar.activation(grouped[:], bank[:].rearrange("p t c -> p c t"), GELU)
            return quantize_h(grouped)

        def hidden_last(banks):
            h = hidden_ring.tile([P, HT, C], BF16, name="h")
            for t in range(HT):
                nc.scalar.activation(h[:, t, :], banks[t][:], GELU)
            grouped = hidden_ring.tile([P, C, HT], BF16, align_bytes=64, name="h_grouped")
            nc.vector.tensor_copy(grouped[:], h[:].rearrange("p t c -> p c t"))
            return quantize_h(grouped)

        def second_product(e, w2_mx, h_mx):
            codes, scales = w2_mx
            if e == LAST:
                sums = [last_psum.tile([P, C], F32, name="last_sums%d" % b)[:] for b in range(NB)]
            else:
                bank = second_psum.tile([P, NB, C], F32, name="second_sums")
                sums = [bank[:, b, :] for b in range(NB)]
            y = hidden_ring.tile([P, NB, C], F32, name="y")
            for b in range(NB):
                cols = slice(b * P, (b + 1) * P)
                nc.tensor.matmul_mx(
                    sums[b],
                    lhsT=codes[:, cols].bitcast(FP8X4),
                    lhsT_scale=scales[:, cols],
                    rhs=h_mx[0][:].bitcast(FP8X4),
                    rhs_scale=h_mx[1][:],
                    start=True,
                    stop=True,
                )
            if e == LAST:
                for b in range(NB):
                    nc.scalar.copy(y[:, b, :], sums[b])
                factors = gates_last[:]
            else:
                nc.scalar.copy(y[:], bank[:])
                factors = gates[:, :, e * C : (e + 1) * C]
            list_cols = offsets[:, e * C // OFFS_COL : (e + 1) * C // OFFS_COL]
            for b in range(NB):
                nc.vector.tensor_tensor(
                    windows[b][:].indirect(list_cols), y[:, b, :], factors[:, b, :], MULT
                )

        chunks = [("x", 0, s) for s in range(PASSES)]
        for e in range(E):
            chunks += [("w1", e, s) for s in range(PASSES)]
            if e == 0:
                chunks.append(("gate", 0, 0))
            chunks.append(("w2", e, 0))
        chunks.append(("gate", LAST, 0))

        def group(chunk, raw):
            kind, e, s = chunk
            if kind == "x":
                return group_x(s, raw)
            if kind == "w1":
                return group_w1(e, s, raw)
            return group_w2(e, raw)

        w1_done = []
        last_banks = []
        h_done = []

        def finish(chunk, grouped):
            kind, e, s = chunk
            if kind == "x":
                quantize_x(s, grouped)
                gather(slot_codes[:, s, :], token_codes[:, s, :])
                if s == SHARED - 1:
                    gather(slot_scales_shared, token_scales_shared[:])
                if s == PASSES - 1:
                    gather(slot_scales_own, token_scales_own[:])
            elif kind == "w2":
                second_product(e, quantize_w2(grouped), h_done[-1])
            elif e == LAST:
                w1_mx = quantize_w1(grouped, 2 if s == PASSES - 1 else 1)
                if s == 0:
                    last_banks.extend(
                        [last_psum.tile([P, C], F32, name="last_sums%d" % t) for t in range(HT)]
                    )
                for t in range(HT):
                    first_product(last_banks[t][:], e, s, t, w1_mx)
                if s == PASSES - 1:
                    h_done.append(hidden_last(last_banks))
            else:
                w1_done.append(quantize_w1(grouped, 1))
                if s == PASSES - 1:
                    h_done.append(hidden(e, w1_done))
                    w1_done.clear()

        raws = [load(chunks[0])]
        nc.sync.dma_start(offsets[:], offs)
        raws += [load(chunk) for chunk in chunks[1:AHEAD]]
        pending = None
        for i, chunk in enumerate(chunks):
            if i + AHEAD < len(chunks):
                raws.append(load(chunks[i + AHEAD]))
            if chunk[0] == "gate":
                continue
            grouped = group(chunk, raws[i])
            if pending is not None:
                finish(*pending)
            pending = (chunk, grouped)
        finish(*pending)

        for b in range(NB):
            nc.sync.dma_start(out[b * P : (b + 1) * P, :], windows[b][:])
